import numpy as np
CORES = [64,65,66,67,68,69,70,71,72,73,74,75,76,77,78,79,80,81,82,83,84,85,86,87,88,89,90,91,92,93,94,95]
N = 32
GROUPS = [[0,1,2,3,4,5,6,7,8,9,10,11,12,13,14,15],[16,17,18,19,20,21,22,23,24,25,26,27,28,29,30,31]]
def setup_inputs(rng):
    return {"x": rng.standard_normal((N, 128, 16), dtype=np.float32)}
def reference(x):
    y = np.empty((N, 128, 16), x.dtype)
    for g in GROUPS:
        n = len(g); b = x.shape[2] // n
        for i, r in enumerate(g):
            y[r] = np.concatenate([x[s][:, i * b:(i + 1) * b] for s in g], axis=1)
    return {"y": y}

@@ -1,0 +1,72 @@
+from concourse.bass import DstId, RemoteDMATransfer
+
+SCRATCH = {
+    "xs": ("sbuf", [128, 16], "float32"),
+    "gw": ("sbuf", [128, 16], "float32"),
+    "land": ("sbuf", [128, 16], "float32"),
+}
+SEMAPHORES = ["loaded", "sent", "staged", "arrived", "stored"]
+
+
+def rank_program(g, core, T, topo):
+    rank = T.rank_of(core)
+    if rank is None:
+        return
+    group = [grp for grp in T.tables["GROUPS"] if rank in grp][0]
+    cores = [T.cores[r] for r in group]
+    idx = {c: j for j, c in enumerate(cores)}
+    me = idx[core]
+    near = [c for c in cores if topo.chip(c) == topo.chip(core)]
+    far = [c for c in cores if topo.chip(c) != topo.chip(core)]
+    mine = [c for c in near if topo.die(c) == topo.die(core)]
+    ports = [c for c in mine if topo.may_write(c, far[0])]
+    share = len(far) // len(ports)
+    ss = mine.index(core)
+    nsrc = len(mine)
+
+    def dst_id(c):
+        rid, pid, _se = topo.addr(c)
+        return DstId(rid=rid, pnc=pid)
+
+    g.sync.dma_start(T.xs[:], T.x[:]).then_inc(T.sem.loaded, 16)
+    g.sync.wait_ge(T.sem.loaded, 16)
+    g.scalar.wait_ge(T.sem.loaded, 16)
+    g.wait_ge(T.sem.loaded, 16)
+
+    g.sync.dma_start(T.land[:, me:me + 1], T.xs[:, me:me + 1]).then_inc(T.sem.arrived, 16)
+
+    transfers = []
+    staged = 0
+    for c in near:
+        if c != core:
+            transfers.append((c, T.land[:, me:me + 1], T.xs[:, idx[c]:idx[c] + 1], T.sem.arrived))
+    for q, port in enumerate(ports):
+        for dd, d in enumerate(far[q * share:(q + 1) * share]):
+            col = dd * nsrc + ss
+            if port == core:
+                g.scalar.dma_start(T.gw[:, col:col + 1], T.xs[:, idx[d]:idx[d] + 1]).then_inc(T.sem.staged, 16)
+                staged += 16
+            else:
+                transfers.append((port, T.gw[:, col:col + 1], T.xs[:, idx[d]:idx[d] + 1], T.sem.staged))
+    g.remote_dma_fused(
+        [RemoteDMATransfer(dst_ids=[dst_id(c)], dma_engine_mask=1 << e, remote_sem=sem, src=src, dst=dst)
+         for e, (c, dst, src, sem) in enumerate(transfers)],
+        local_sem=T.sem.sent)
+    sent = len(transfers)
+
+    if core in ports:
+        q = ports.index(core)
+        staged += (nsrc - 1) * share
+        g.wait_ge(T.sem.staged, staged)
+        base = idx[mine[0]]
+        g.remote_dma_fused(
+            [RemoteDMATransfer(dst_ids=[dst_id(d)], dma_engine_mask=3 << (2 * dd), remote_sem=T.sem.arrived,
+                               src=T.gw[:, dd * nsrc:(dd + 1) * nsrc], dst=T.land[:, base:base + nsrc])
+             for dd, d in enumerate(far[q * share:(q + 1) * share])],
+            local_sem=T.sem.sent)
+        sent += 2 * share
+    g.wait_ge(T.sem.sent, sent)
+
+    g.sync.wait_ge(T.sem.arrived, 16 + (len(near) - 1) + 2 * 2)
+    g.sync.dma_start(T.y[:], T.land[:]).then_inc(T.sem.stored, 16)
+    g.sync.wait_ge(T.sem.stored, 16)

@@ -5,7 +5,7 @@ SCRATCH = {
     "gw": ("sbuf", [128, 16], "float32"),
     "land": ("sbuf", [128, 16], "float32"),
 }
-SEMAPHORES = ["loaded", "sent", "staged", "arrived", "stored"]
+SEMAPHORES = ["loaded", "sent", "staged", "own", "arrived", "stored"]
 
 
 def rank_program(g, core, T, topo):
@@ -30,23 +30,18 @@ def rank_program(g, core, T, topo):
 
     g.sync.dma_start(T.xs[:], T.x[:]).then_inc(T.sem.loaded, 16)
     g.sync.wait_ge(T.sem.loaded, 16)
-    g.scalar.wait_ge(T.sem.loaded, 16)
     g.wait_ge(T.sem.loaded, 16)
 
     g.sync.dma_start(T.land[:, me:me + 1], T.xs[:, me:me + 1]).then_inc(T.sem.arrived, 16)
 
     transfers = []
-    staged = 0
     for c in near:
         if c != core:
             transfers.append((c, T.land[:, me:me + 1], T.xs[:, idx[c]:idx[c] + 1], T.sem.arrived))
     for q, port in enumerate(ports):
-        for dd, d in enumerate(far[q * share:(q + 1) * share]):
-            col = dd * nsrc + ss
-            if port == core:
-                g.scalar.dma_start(T.gw[:, col:col + 1], T.xs[:, idx[d]:idx[d] + 1]).then_inc(T.sem.staged, 16)
-                staged += 16
-            else:
+        if port != core:
+            for dd, d in enumerate(far[q * share:(q + 1) * share]):
+                col = dd * nsrc + ss
                 transfers.append((port, T.gw[:, col:col + 1], T.xs[:, idx[d]:idx[d] + 1], T.sem.staged))
     g.remote_dma_fused(
         [RemoteDMATransfer(dst_ids=[dst_id(c)], dma_engine_mask=1 << e, remote_sem=sem, src=src, dst=dst)
@@ -56,13 +51,17 @@ def rank_program(g, core, T, topo):
 
     if core in ports:
         q = ports.index(core)
-        staged += (nsrc - 1) * share
-        g.wait_ge(T.sem.staged, staged)
+        served = far[q * share:(q + 1) * share]
+        f0 = idx[served[0]]
+        g.dma_start(T.gw[:, ss:share * nsrc:nsrc], T.xs[:, f0:f0 + share],
+                    allow_slow_non_contiguous=True).then_inc(T.sem.own, 16)
+        g.wait_ge(T.sem.own, 16)
+        g.wait_ge(T.sem.staged, (nsrc - 1) * share)
         base = idx[mine[0]]
         g.remote_dma_fused(
             [RemoteDMATransfer(dst_ids=[dst_id(d)], dma_engine_mask=3 << (2 * dd), remote_sem=T.sem.arrived,
                                src=T.gw[:, dd * nsrc:(dd + 1) * nsrc], dst=T.land[:, base:base + nsrc])
-             for dd, d in enumerate(far[q * share:(q + 1) * share])],
+             for dd, d in enumerate(served)],
             local_sem=T.sem.sent)
         sent += 2 * share
     g.wait_ge(T.sem.sent, sent)

from concourse.bass import DstId, RemoteDMATransfer

SCRATCH = {
    "xs": ("sbuf", [128, 16], "float32"),
    "gw": ("sbuf", [128, 16], "float32"),
    "land": ("sbuf", [128, 16], "float32"),
}
SEMAPHORES = ["loaded", "sent", "staged", "own", "arrived", "stored"]


def rank_program(g, core, T, topo):
    rank = T.rank_of(core)
    if rank is None:
        return
    group = [grp for grp in T.tables["GROUPS"] if rank in grp][0]
    cores = [T.cores[r] for r in group]
    idx = {c: j for j, c in enumerate(cores)}
    me = idx[core]
    near = [c for c in cores if topo.chip(c) == topo.chip(core)]
    far = [c for c in cores if topo.chip(c) != topo.chip(core)]
    mine = [c for c in near if topo.die(c) == topo.die(core)]
    ports = [c for c in mine if topo.may_write(c, far[0])]
    share = len(far) // len(ports)
    ss = mine.index(core)
    nsrc = len(mine)

    def dst_id(c):
        rid, pid, _se = topo.addr(c)
        return DstId(rid=rid, pnc=pid)

    g.sync.dma_start(T.xs[:], T.x[:]).then_inc(T.sem.loaded, 16)
    g.sync.wait_ge(T.sem.loaded, 16)
    g.wait_ge(T.sem.loaded, 16)

    g.sync.dma_start(T.land[:, me:me + 1], T.xs[:, me:me + 1]).then_inc(T.sem.arrived, 16)

    transfers = []
    for c in near:
        if c != core:
            transfers.append((c, T.land[:, me:me + 1], T.xs[:, idx[c]:idx[c] + 1], T.sem.arrived))
    for q, port in enumerate(ports):
        if port != core:
            for dd, d in enumerate(far[q * share:(q + 1) * share]):
                col = dd * nsrc + ss
                transfers.append((port, T.gw[:, col:col + 1], T.xs[:, idx[d]:idx[d] + 1], T.sem.staged))
    g.remote_dma_fused(
        [RemoteDMATransfer(dst_ids=[dst_id(c)], dma_engine_mask=1 << e, remote_sem=sem, src=src, dst=dst)
         for e, (c, dst, src, sem) in enumerate(transfers)],
        local_sem=T.sem.sent)
    sent = len(transfers)

    if core in ports:
        q = ports.index(core)
        served = far[q * share:(q + 1) * share]
        f0 = idx[served[0]]
        g.dma_start(T.gw[:, ss:share * nsrc:nsrc], T.xs[:, f0:f0 + share],
                    allow_slow_non_contiguous=True).then_inc(T.sem.own, 16)
        g.wait_ge(T.sem.own, 16)
        g.wait_ge(T.sem.staged, (nsrc - 1) * share)
        base = idx[mine[0]]
        g.remote_dma_fused(
            [RemoteDMATransfer(dst_ids=[dst_id(d)], dma_engine_mask=3 << (2 * dd), remote_sem=T.sem.arrived,
                               src=T.gw[:, dd * nsrc:(dd + 1) * nsrc], dst=T.land[:, base:base + nsrc])
             for dd, d in enumerate(served)],
            local_sem=T.sem.sent)
        sent += 2 * share
    g.wait_ge(T.sem.sent, sent)

    g.sync.wait_ge(T.sem.arrived, 16 + (len(near) - 1) + 2 * 2)
    g.sync.dma_start(T.y[:], T.land[:]).then_inc(T.sem.stored, 16)
    g.sync.wait_ge(T.sem.stored, 16)
